import numpy as np
import ml_dtypes


def mxq(x, axis, fmt="e4m3"):
    dtype, down = {"e4m3": (ml_dtypes.float8_e4m3fn, 7), "e5m2": (ml_dtypes.float8_e5m2, 14)}[fmt]
    v = np.moveaxis(np.asarray(x, np.float32).astype(ml_dtypes.bfloat16).astype(np.float64), axis, -1)
    blocks = v.reshape(v.shape[:-1] + (-1, 32))
    amax = np.abs(blocks).max(-1, keepdims=True)
    byte = np.maximum(np.where(amax > 0, np.frexp(amax)[1] - 1 + 127, 0) - down, 1)
    scale = np.exp2(byte - 127.0)
    codes = (blocks / scale).astype(np.float32).astype(dtype).astype(np.float64)
    return np.moveaxis((codes * scale).reshape(v.shape), -1, axis)


WIDE = False


def mx_kscale(k):
    if not WIDE:
        return np.ones(k)
    levels = np.array([10, -10, 5, -5, 0])
    if k % 512:
        return np.exp2(np.random.permutation(np.resize(levels, k // 32))).repeat(32)
    a = np.empty((k // 512, 16))
    for p in range(k // 512):
        a[p, :8] = np.random.permutation(np.resize(levels, 8))
        for g in range(8):
            far = levels[np.abs(levels - a[p, g]) >= 10]
            a[p, g + 8] = far[np.random.randint(len(far))]
    return np.exp2(a.ravel()).repeat(32)


def f64(x):
    return np.asarray(x).astype(np.float64)


def striped(idx):
    return np.tile(idx.reshape(-1, 16).T, (8, 1)).astype(np.uint16)


def unstriped(offs):
    return offs[:16].T.reshape(-1).astype(np.int64)


def pack_weight(w):
    k, n = w.shape
    w = f64(np.asarray(w, np.float32).astype(ml_dtypes.bfloat16)).reshape(k // 32, 32, n)
    amax = np.abs(w).max(1)
    byte = np.clip(np.where(amax > 0, np.frexp(amax)[1] - 1 + 127 - 7, 1), 1, 254)
    scaled = (w * np.exp2(127.0 - byte)[:, None, :]).reshape(k, n).astype(np.float32)
    words = np.ascontiguousarray(scaled.reshape(k // 512, 128, 4, n).transpose(0, 1, 3, 2)).astype(ml_dtypes.float8_e4m3fn).view(np.uint8)
    return words, np.ascontiguousarray(byte.astype(np.uint8).reshape(k // 512, 16, n))


def unpack_weight(words, scales):
    g, p, n, _ = words.shape
    vals = np.ascontiguousarray(words).view(ml_dtypes.float8_e4m3fn).astype(np.float64) * np.repeat(np.exp2(scales.astype(np.float64) - 127.0), 8, axis=1)[..., None]
    return vals.transpose(0, 1, 3, 2).reshape(g * 512, n)


def sigmoid(v):
    return 1.0 / (1.0 + np.exp(-np.maximum(v, -700.0)))

def planes(y):
    n, m = y.shape
    v = y.astype(np.float32).astype(ml_dtypes.bfloat16).astype(np.float64).reshape(n // 32, 32, m)
    top = np.abs(v).max(1)
    byte = np.clip(np.where(top > 0, np.frexp(top)[1] - 1 + 127 - 7, 1), 1, 254)
    codes = (v * np.exp2(127.0 - byte)[:, None, :]).reshape(n, m).astype(np.float32).astype(ml_dtypes.float8_e4m3fn).view(np.uint8)
    words = codes.reshape(n // 512, 128, 4, m).transpose(0, 1, 3, 2)
    return np.ascontiguousarray(words), np.ascontiguousarray(byte.astype(np.uint8).reshape(n // 512, 16, m))


K, T, N = 512, 512, 512


def setup_inputs():
    n = np.random.standard_normal
    s = mx_kscale(K)[:, None]
    packed_xT = pack_weight(n((K, T)) * s)
    return {
        "x_words": packed_xT[0],
        "x_scales": packed_xT[1],
        "w1": (n((K, N)) / np.sqrt(K) / s).astype(np.float32),
        "w2": (n((K, N)) / np.sqrt(K) / s).astype(np.float32),
        "w3": (n((K, N)) / np.sqrt(K) / s).astype(np.float32),
        "pos1": striped(np.random.permutation(T)),
        "pos2": striped(np.random.permutation(T)),
        "pos3": striped(np.random.permutation(T)),
        "pos4": striped(np.random.permutation(T)),
    }


def reference(x_words, x_scales, w1, w2, w3, pos1, pos2, pos3, pos4):
    xq = unpack_weight(x_words, x_scales)
    y = mxq(f64(w1), 0, "e4m3").T @ xq
    e = mxq(f64(w2), 0, "e4m3").T @ xq
    h = mxq(f64(w3), 0, "e4m3").T @ xq
    z = (sigmoid(y + e[:, unstriped(pos1)])) * h[:, unstriped(pos1)] + (sigmoid(y + e[:, unstriped(pos2)])) * h[:, unstriped(pos2)] + (sigmoid(y + e[:, unstriped(pos3)])) * h[:, unstriped(pos3)] + (sigmoid(y + e[:, unstriped(pos4)])) * h[:, unstriped(pos4)]
    out_0 = z
    return (out_0,) + planes(out_0)

@@ -1,0 +1,227 @@
+from contextlib import ExitStack
+
+import concourse.mybir as mybir
+from concourse.masks import make_identity
+
+K, T, N, D = 512, 512, 512, 4
+FLOPS = 3 * 2 * K * T * N
+
+F32 = mybir.dt.float32
+BF16 = mybir.dt.bfloat16
+I32 = mybir.dt.int32
+U32 = mybir.dt.uint32
+U16 = mybir.dt.uint16
+U8 = mybir.dt.uint8
+FP8X4 = mybir.dt.float8_e4m3fn_x4
+ADD = mybir.AluOpType.add
+MULT = mybir.AluOpType.mult
+SIGMOID = mybir.ActivationFunctionType.Sigmoid
+
+P = 128
+PACK = 4
+BLOCKS = N // P
+CHUNKS = T // P
+SPARE = 8
+QUAD = 32
+
+
+def tile_picked_wgatedg_none_lo_kernel(
+    tc, x_words, x_scales, w1, w2, w3, pos1, pos2, pos3, pos4, out_0, out_1, out_2
+):
+    nc = tc.nc
+    with ExitStack() as ctx:
+        keep = ctx.enter_context(tc.tile_pool(name="keep", bufs=1))
+        work = ctx.enter_context(tc.tile_pool(name="work", bufs=2))
+        psum = ctx.enter_context(tc.psum_pool(name="psum", bufs=1))
+
+        x_codes = keep.tile([P, T], U32, align_bytes=64)
+        x_plane = keep.tile([P, T], U8, align_bytes=64)
+        lists = [keep.tile([P, T // 16], U16, name="list%d" % d) for d in range(D)]
+        weights = {"e": w2, "y": w1, "h": w3}
+        raw = {}
+        for b in range(BLOCKS):
+            for part in weights:
+                raw[part, b] = keep.tile([P, PACK, P], F32, name="raw_%s%d" % (part, b))
+
+        def load_weight(part, b):
+            cols = weights[part][:, b * P : (b + 1) * P]
+            nc.sync.dma_start(out=raw[part, b][:], in_=cols.rearrange("(p j) m -> p j m", j=PACK))
+
+        for q in range(P // QUAD):
+            nc.sync.dma_start(
+                out=x_plane[QUAD * q : QUAD * q + 4, :].bitcast(I32),
+                in_=x_scales[0, 4 * q : 4 * q + 4, :].bitcast(I32),
+            )
+        load_weight("e", 0)
+        load_weight("y", 0)
+        nc.sync.dma_start(
+            out=x_codes[:].bitcast(I32), in_=x_words[0].rearrange("p n t -> p (n t)").bitcast(I32)
+        )
+        load_weight("h", 0)
+        nc.sync.dma_start(lists[0][:], pos1)
+        nc.sync.dma_start(lists[1][:], pos2)
+        nc.sync.dma_start(lists[2][:], pos3)
+        nc.sync.dma_start(lists[3][:], pos4)
+        for b in range(1, BLOCKS):
+            for part in weights:
+                load_weight(part, b)
+
+        ident = keep.tile([P, P], F32)
+        make_identity(nc, ident[:])
+
+        proj = {}
+        for b in range(BLOCKS):
+            proj["y", b] = keep.tile([P, T], F32, name="y%d" % b)
+            for part in ("e", "h"):
+                proj[part, b] = keep.tile([P, T + SPARE], F32, name="%s%d" % (part, b))
+
+        z_codes = keep.tile([P, T], U32, align_bytes=64)
+        z_plane = keep.tile([P, T], U8, align_bytes=64)
+        pairs = [keep.tile([P, 2, P, 2], BF16, name="pairs%d" % c) for c in range(CHUNKS)]
+
+        warm = keep.tile([P, 1], F32)
+        nc.scalar.activation(warm[:], ident[:, 0:1], SIGMOID)
+
+        def project(part, b, round_copy, out_copy):
+            grouped = work.tile([P, P, PACK], BF16, align_bytes=64, bufs=3)
+            round_copy(
+                out=grouped[:].rearrange("p (c i) j -> p c j i", i=4),
+                in_=raw[part, b][:].rearrange("p j (c i) -> p c j i", i=4),
+            )
+            w_codes = work.tile([P, P], U32, align_bytes=64, bufs=3)
+            w_plane = work.tile([P, P], U8, align_bytes=64, bufs=3)
+            nc.vector.quantize_mx(
+                out=w_codes[:].bitcast(FP8X4),
+                scales=w_plane[:],
+                in_=grouped[:].rearrange("p c j -> p (c j)"),
+            )
+            acc = psum.tile([P, T], F32, tag="bank", bufs=4)
+            nc.tensor.matmul_mx(
+                out=acc[:],
+                lhsT=w_codes[:].bitcast(FP8X4),
+                lhsT_scale=w_plane[:],
+                rhs=x_codes[:].bitcast(FP8X4),
+                rhs_scale=x_plane[:],
+                start=True,
+                stop=True,
+            )
+            out_copy(out=proj[part, b][:, :T], in_=acc[:])
+
+        gates = {}
+        sums = {}
+
+        def gate(b, d):
+            logit = work.tile([P, T], F32, bufs=3)
+            nc.vector.tensor_tensor(logit[:], proj["e", b][:].indirect(lists[d][:]), proj["y", b][:], ADD)
+            gates[b, d] = work.tile([P, T], F32, bufs=3, name="gate")
+            nc.scalar.activation(gates[b, d][:], logit[:], SIGMOID)
+
+        def message(b, d, chunks):
+            width = len(chunks) * P
+            first = chunks[0] * P
+            msg = work.tile([P, width], F32, bufs=3)
+            offs = lists[d][:, first // 16 : (first + width) // 16]
+            nc.vector.tensor_tensor(
+                msg[:], proj["h", b][:].indirect(offs), gates[b, d][:, first : first + width], MULT
+            )
+            for i, c in enumerate(chunks):
+                if d == 0:
+                    sums[b, c] = psum.tile([P, P], F32, name="sum%d" % c)
+                nc.tensor.matmul(
+                    sums[b, c][:],
+                    msg[:, i * P : (i + 1) * P],
+                    ident[:],
+                    start=(d == 0),
+                    stop=(d == D - 1),
+                    is_transpose=True,
+                )
+            return msg
+
+        exact = {}
+
+        def drain_pairs(b, c):
+            nc.scalar.copy(
+                out=pairs[c][:, :, QUAD * b : QUAD * (b + 1), :],
+                in_=sums[b, c][:].rearrange("v (l u e) -> v u l e", u=2, e=2),
+            )
+
+        def drain_exact(b, c, copy):
+            exact[b, c] = work.tile([P, P], F32, name="exact", bufs=6)
+            copy(out=exact[b, c][:], in_=sums[b, c][:])
+
+        def drain(b, chunks):
+            for c in chunks:
+                drain_pairs(b, c)
+                drain_exact(b, c, nc.scalar.copy)
+
+        def store_rows(b, chunks):
+            width = len(chunks) * P
+            first = chunks[0] * P
+            row_bank = psum.tile([P, width], F32, tag="bank", bufs=4)
+            for i, c in enumerate(chunks):
+                nc.tensor.transpose(row_bank[:, i * P : (i + 1) * P], exact[b, c][:], ident[:])
+            z_rows = work.tile([P, width], F32)
+            nc.scalar.copy(out=z_rows[:], in_=row_bank[:])
+            nc.sync.dma_start(out=out_0[b * P : (b + 1) * P, first : first + width], in_=z_rows[:])
+
+        def requantize(c, word_copy):
+            pair_words = pairs[c][:].rearrange("v u l e -> v u (l e)").bitcast(F32)
+            word_bank = psum.tile([P, 2, P], F32, tag="bank", bufs=4)
+            for u in range(2):
+                nc.tensor.transpose(word_bank[:, u, :], pair_words[:, u, :], ident[:])
+            z_grouped = work.tile([P, P * PACK], BF16, align_bytes=64, bufs=4)
+            word_copy(
+                out=z_grouped[:].bitcast(F32).rearrange("p (v u) -> p v u", u=2),
+                in_=word_bank[:].rearrange("p u v -> p v u"),
+            )
+            cols = slice(c * P, (c + 1) * P)
+            nc.vector.quantize_mx(out=z_codes[:, cols].bitcast(FP8X4), scales=z_plane[:, cols], in_=z_grouped[:])
+
+        out_words = out_1[0].rearrange("l v t -> l (v t)").bitcast(I32)
+
+        def store_words(chunks):
+            cols = slice(chunks[0] * P, (chunks[-1] + 1) * P)
+            nc.sync.dma_start(out=out_words[:, cols], in_=z_codes[:, cols].bitcast(I32))
+
+        project("e", 0, nc.vector.tensor_copy, nc.vector.tensor_copy)
+        project("y", 0, nc.vector.tensor_copy, nc.vector.tensor_copy)
+
+        every = list(range(CHUNKS))
+        last = BLOCKS - 1
+        steps = [(b, d) for b in range(BLOCKS) for d in range(D)]
+        for s, (b, d) in enumerate(steps):
+            gate(b, d)
+            if s == 0:
+                project("h", 0, nc.scalar.copy, nc.scalar.copy)
+            if 0 < s < len(steps) - 1:
+                message(*steps[s - 1], every)
+            if b < last and d < 3:
+                project("eyh"[d], b + 1, nc.scalar.copy, nc.scalar.copy)
+            if b > 0 and d == 0:
+                drain(b - 1, every)
+            if b > 0 and d == 1:
+                store_rows(b - 1, every)
+
+        message(last, 2, [0, 1])
+        message(last, 3, [0, 1])
+        drain(last, [0, 1])
+        message(last, 2, [2, 3])
+        requantize(0, nc.scalar.copy)
+        requantize(1, nc.scalar.copy)
+        store_words([0, 1])
+        store_rows(last, [0, 1])
+        message(last, 3, [2])
+        drain_pairs(last, 2)
+        final = message(last, 3, [3])
+        drain_pairs(last, 3)
+        drain_exact(last, 2, nc.vector.tensor_copy)
+        drain_exact(last, 3, nc.vector.tensor_copy)
+        requantize(2, nc.vector.tensor_copy)
+        requantize(3, nc.scalar.copy)
+        store_words([2, 3])
+        store_rows(last, [2, 3])
+        for q in range(P // QUAD):
+            nc.scalar.dma_start(
+                out=out_2[0, 4 * q : 4 * q + 4, :].bitcast(I32),
+                in_=z_plane[QUAD * q : QUAD * q + 4, :].bitcast(I32),
+            )

@@ -23,6 +23,9 @@ BLOCKS = N // P
 CHUNKS = T // P
 SPARE = 8
 QUAD = 32
+HALF = T // 2
+ROUND_SLOT = {("h", 0): "slot_a", ("ey", 1): "slot_b"}
+CODES_SLOT = {("y", 0): "slot_a", ("h", 0): "slot_b"}
 
 
 def tile_picked_wgatedg_none_lo_kernel(
@@ -53,12 +56,12 @@ def tile_picked_wgatedg_none_lo_kernel(
                 in_=x_scales[0, 4 * q : 4 * q + 4, :].bitcast(I32),
             )
         load_weight("e", 0)
-        load_weight("y", 0)
         nc.sync.dma_start(
             out=x_codes[:].bitcast(I32), in_=x_words[0].rearrange("p n t -> p (n t)").bitcast(I32)
         )
-        load_weight("h", 0)
+        load_weight("y", 0)
         nc.sync.dma_start(lists[0][:], pos1)
+        load_weight("h", 0)
         nc.sync.dma_start(lists[1][:], pos2)
         nc.sync.dma_start(lists[2][:], pos3)
         nc.sync.dma_start(lists[3][:], pos4)
@@ -77,95 +80,126 @@ def tile_picked_wgatedg_none_lo_kernel(
 
         z_codes = keep.tile([P, T], U32, align_bytes=64)
         z_plane = keep.tile([P, T], U8, align_bytes=64)
-        pairs = [keep.tile([P, 2, P, 2], BF16, name="pairs%d" % c) for c in range(CHUNKS)]
+        pairs = keep.tile([P, CHUNKS, 2, P, 2], BF16)
 
-        warm = keep.tile([P, 1], F32)
-        nc.scalar.activation(warm[:], ident[:, 0:1], SIGMOID)
 
-        def project(part, b, round_copy, out_copy):
-            grouped = work.tile([P, P, PACK], BF16, align_bytes=64, bufs=3)
-            round_copy(
-                out=grouped[:].rearrange("p (c i) j -> p c j i", i=4),
-                in_=raw[part, b][:].rearrange("p j (c i) -> p c j i", i=4),
-            )
-            w_codes = work.tile([P, P], U32, align_bytes=64, bufs=3)
-            w_plane = work.tile([P, P], U8, align_bytes=64, bufs=3)
+        rounded = {}
+        quantized = {}
+        products = {}
+
+        def round_weights(parts, b, copy):
+            grouped = keep.tile([P, len(parts), P, PACK], BF16, align_bytes=64, tag=ROUND_SLOT.get((parts, b), "rounded_%s%d" % (parts, b)))
+            for i, part in enumerate(parts):
+                copy(
+                    out=grouped[:, i].rearrange("p (c i) j -> p c j i", i=4),
+                    in_=raw[part, b][:].rearrange("p j (c i) -> p c j i", i=4),
+                )
+            rounded[parts, b] = grouped
+
+        def quantize_weights(parts, b):
+            w_codes = keep.tile([P, len(parts) * P], U32, align_bytes=64, tag=CODES_SLOT.get((parts, b), "codes_%s%d" % (parts, b)))
+            w_plane = work.tile([P, len(parts) * P], U8, align_bytes=64, bufs=9)
             nc.vector.quantize_mx(
                 out=w_codes[:].bitcast(FP8X4),
                 scales=w_plane[:],
-                in_=grouped[:].rearrange("p c j -> p (c j)"),
+                in_=rounded[parts, b][:].rearrange("p i c j -> p (i c j)"),
             )
-            acc = psum.tile([P, T], F32, tag="bank", bufs=4)
+            for i, part in enumerate(parts):
+                quantized[part, b] = (w_codes[:, i * P : (i + 1) * P], w_plane[:, i * P : (i + 1) * P])
+
+        def multiply(part, b, cols):
+            w_codes, w_plane = quantized[part, b]
+            acc = psum.tile([P, cols.stop - cols.start], F32, tag="bank", bufs=4)
             nc.tensor.matmul_mx(
                 out=acc[:],
-                lhsT=w_codes[:].bitcast(FP8X4),
-                lhsT_scale=w_plane[:],
-                rhs=x_codes[:].bitcast(FP8X4),
-                rhs_scale=x_plane[:],
+                lhsT=w_codes.bitcast(FP8X4),
+                lhsT_scale=w_plane,
+                rhs=x_codes[:, cols].bitcast(FP8X4),
+                rhs_scale=x_plane[:, cols],
                 start=True,
                 stop=True,
             )
-            out_copy(out=proj[part, b][:, :T], in_=acc[:])
+            products[part, b, cols.start] = acc
+
+        def unload(part, b, cols, copy):
+            copy(out=proj[part, b][:, cols], in_=products[part, b, cols.start][:])
+
+        def offsets(d, cols):
+            return lists[d][:, cols.start // 16 : cols.stop // 16]
 
         gates = {}
+        messages = {}
         sums = {}
 
-        def gate(b, d):
+        def gate(b, d, pieces):
             logit = work.tile([P, T], F32, bufs=3)
-            nc.vector.tensor_tensor(logit[:], proj["e", b][:].indirect(lists[d][:]), proj["y", b][:], ADD)
-            gates[b, d] = work.tile([P, T], F32, bufs=3, name="gate")
+            for cols in pieces:
+                nc.vector.tensor_tensor(
+                    logit[:, cols], proj["e", b][:].indirect(offsets(d, cols)), proj["y", b][:, cols], ADD
+                )
+            gates[b, d] = work.tile([P, T], F32, bufs=4, name="gate")
             nc.scalar.activation(gates[b, d][:], logit[:], SIGMOID)
 
         def message(b, d, chunks):
-            width = len(chunks) * P
-            first = chunks[0] * P
-            msg = work.tile([P, width], F32, bufs=3)
-            offs = lists[d][:, first // 16 : (first + width) // 16]
+            cols = slice(chunks[0] * P, (chunks[-1] + 1) * P)
+            msg = work.tile([P, len(chunks) * P], F32, bufs=20)
             nc.vector.tensor_tensor(
-                msg[:], proj["h", b][:].indirect(offs), gates[b, d][:, first : first + width], MULT
+                msg[:], proj["h", b][:].indirect(offsets(d, cols)), gates[b, d][:, cols], MULT
             )
             for i, c in enumerate(chunks):
-                if d == 0:
-                    sums[b, c] = psum.tile([P, P], F32, name="sum%d" % c)
-                nc.tensor.matmul(
-                    sums[b, c][:],
-                    msg[:, i * P : (i + 1) * P],
-                    ident[:],
-                    start=(d == 0),
-                    stop=(d == D - 1),
-                    is_transpose=True,
-                )
+                messages[b, d, c] = msg[:, i * P : (i + 1) * P]
             return msg
+
+        def accumulate(b, d, c, start, stop):
+            nc.tensor.matmul(sums[b, c], messages[b, d, c], ident[:], start=start, stop=stop, is_transpose=True)
+
+        def block_message(b, d):
+            message(b, d, every)
+            if d == D - 2:
+                sums[b] = psum.tile([P, CHUNKS, P], F32, name="sum%d" % (b + 1))
+                for turn in (d, 0, 1):
+                    for c in range(CHUNKS):
+                        sums[b, c] = sums[b][:, c, :]
+                        accumulate(b, turn, c, turn == d and c == 0, False)
+            if d == D - 1:
+                for c in range(CHUNKS):
+                    accumulate(b, d, c, False, c == CHUNKS - 1)
 
         exact = {}
 
+        def drain_block(b):
+            tile = work.tile([P, CHUNKS, P], F32, name="exact_block")
+            nc.scalar.copy(out=tile[:], in_=sums[b][:])
+            for c in range(CHUNKS):
+                exact[b, c] = tile[:, c, :]
+            nc.scalar.copy(
+                out=pairs[:, :, :, QUAD * b : QUAD * (b + 1), :],
+                in_=sums[b][:].rearrange("v c (l u e) -> v c u l e", u=2, e=2),
+            )
+
         def drain_pairs(b, c):
             nc.scalar.copy(
-                out=pairs[c][:, :, QUAD * b : QUAD * (b + 1), :],
-                in_=sums[b, c][:].rearrange("v (l u e) -> v u l e", u=2, e=2),
+                out=pairs[:, c, :, QUAD * b : QUAD * (b + 1), :],
+                in_=sums[b, c].rearrange("v (l u e) -> v u l e", u=2, e=2),
             )
 
         def drain_exact(b, c, copy):
-            exact[b, c] = work.tile([P, P], F32, name="exact", bufs=6)
-            copy(out=exact[b, c][:], in_=sums[b, c][:])
-
-        def drain(b, chunks):
-            for c in chunks:
-                drain_pairs(b, c)
-                drain_exact(b, c, nc.scalar.copy)
+            tile = work.tile([P, P], F32, name="exact_chunk", bufs=4)
+            copy(out=tile[:], in_=sums[b, c])
+            exact[b, c] = tile[:]
 
         def store_rows(b, chunks):
             width = len(chunks) * P
             first = chunks[0] * P
             row_bank = psum.tile([P, width], F32, tag="bank", bufs=4)
             for i, c in enumerate(chunks):
-                nc.tensor.transpose(row_bank[:, i * P : (i + 1) * P], exact[b, c][:], ident[:])
+                nc.tensor.transpose(row_bank[:, i * P : (i + 1) * P], exact[b, c], ident[:])
             z_rows = work.tile([P, width], F32)
             nc.scalar.copy(out=z_rows[:], in_=row_bank[:])
             nc.sync.dma_start(out=out_0[b * P : (b + 1) * P, first : first + width], in_=z_rows[:])
 
         def requantize(c, word_copy):
-            pair_words = pairs[c][:].rearrange("v u l e -> v u (l e)").bitcast(F32)
+            pair_words = pairs[:, c].rearrange("v u l e -> v u (l e)").bitcast(F32)
             word_bank = psum.tile([P, 2, P], F32, tag="bank", bufs=4)
             for u in range(2):
                 nc.tensor.transpose(word_bank[:, u, :], pair_words[:, u, :], ident[:])
@@ -183,45 +217,88 @@ def tile_picked_wgatedg_none_lo_kernel(
             cols = slice(chunks[0] * P, (chunks[-1] + 1) * P)
             nc.sync.dma_start(out=out_words[:, cols], in_=z_codes[:, cols].bitcast(I32))
 
-        project("e", 0, nc.vector.tensor_copy, nc.vector.tensor_copy)
-        project("y", 0, nc.vector.tensor_copy, nc.vector.tensor_copy)
-
+        whole = slice(0, T)
+        halves = [slice(0, HALF), slice(HALF, T)]
         every = list(range(CHUNKS))
         last = BLOCKS - 1
-        steps = [(b, d) for b in range(BLOCKS) for d in range(D)]
-        for s, (b, d) in enumerate(steps):
-            gate(b, d)
-            if s == 0:
-                project("h", 0, nc.scalar.copy, nc.scalar.copy)
-            if 0 < s < len(steps) - 1:
-                message(*steps[s - 1], every)
-            if b < last and d < 3:
-                project("eyh"[d], b + 1, nc.scalar.copy, nc.scalar.copy)
-            if b > 0 and d == 0:
-                drain(b - 1, every)
-            if b > 0 and d == 1:
-                store_rows(b - 1, every)
 
-        message(last, 2, [0, 1])
-        message(last, 3, [0, 1])
-        drain(last, [0, 1])
-        message(last, 2, [2, 3])
+        round_weights("e", 0, nc.vector.tensor_copy)
+        quantize_weights("e", 0)
+        round_weights("y", 0, nc.vector.tensor_copy)
+        quantize_weights("y", 0)
+        multiply("e", 0, whole)
+        unload("e", 0, whole, nc.scalar.copy)
+        for cols in halves:
+            multiply("y", 0, cols)
+            unload("y", 0, cols, nc.scalar.copy)
+
+        def last_message(d, chunks):
+            msg = message(last, d, chunks)
+            for c in chunks:
+                if d == 0:
+                    sums[last, c] = psum.tile([P, P], F32, name="sum%d" % c)[:]
+                accumulate(last, d, c, d == 0, d == D - 1)
+            return msg
+
+        for b in range(BLOCKS):
+            for d in range(D):
+                gate(b, d, halves if b == 0 and d == 0 else [whole])
+                if b == 0 and d == 0:
+                    round_weights("h", 0, nc.scalar.copy)
+                    quantize_weights("h", 0)
+                    multiply("h", 0, whole)
+                    unload("h", 0, whole, nc.scalar.copy)
+                if d < 2 and b > 0:
+                    block_message(b - 1, d + 2)
+                elif d >= 2 and b < last:
+                    block_message(b, d - 2)
+                elif d >= 2:
+                    last_message(d - 2, every if d == 2 else every[:-1])
+                if b < last:
+                    if d == 0:
+                        round_weights("ey", b + 1, nc.scalar.copy)
+                    if d == 1:
+                        quantize_weights("ey", b + 1)
+                        multiply("e", b + 1, whole)
+                        multiply("y", b + 1, whole)
+                        round_weights("h", b + 1, nc.scalar.copy)
+                    if d == 2:
+                        unload("e", b + 1, whole, nc.scalar.copy)
+                        unload("y", b + 1, whole, nc.scalar.copy)
+                        quantize_weights("h", b + 1)
+                        multiply("h", b + 1, whole)
+                    if d == 3:
+                        unload("h", b + 1, whole, nc.scalar.copy)
+                if b > 0 and d == 2:
+                    drain_block(b - 1)
+                if b > 0 and d == 3:
+                    store_rows(b - 1, every)
+
+        last_message(2, [0, 1])
+        last_message(3, [0, 1])
+        for c in (0, 1):
+            drain_pairs(last, c)
+            drain_exact(last, c, nc.scalar.copy)
+        last_message(2, [2])
+        last_message(3, [2])
         requantize(0, nc.scalar.copy)
         requantize(1, nc.scalar.copy)
-        store_words([0, 1])
-        store_rows(last, [0, 1])
-        message(last, 3, [2])
         drain_pairs(last, 2)
-        final = message(last, 3, [3])
-        drain_pairs(last, 3)
-        drain_exact(last, 2, nc.vector.tensor_copy)
-        drain_exact(last, 3, nc.vector.tensor_copy)
+        drain_exact(last, 2, nc.scalar.copy)
+        last_message(1, [3])
+        last_message(2, [3])
+        last_message(3, [3])
         requantize(2, nc.vector.tensor_copy)
+        store_rows(last, [0, 1, 2])
+        store_words([0, 1, 2])
+        drain_pairs(last, 3)
+        drain_exact(last, 3, nc.vector.tensor_copy)
         requantize(3, nc.scalar.copy)
-        store_words([2, 3])
-        store_rows(last, [2, 3])
+        store_words([3])
+        store_rows(last, [3])
         for q in range(P // QUAD):
-            nc.scalar.dma_start(
+            queue = nc.sync if q % 2 else nc.scalar
+            queue.dma_start(
                 out=out_2[0, 4 * q : 4 * q + 4, :].bitcast(I32),
                 in_=z_plane[QUAD * q : QUAD * q + 4, :].bitcast(I32),
             )

@@ -50,12 +50,12 @@ def tile_picked_wgatedg_none_lo_kernel(
             cols = weights[part][:, b * P : (b + 1) * P]
             nc.sync.dma_start(out=raw[part, b][:], in_=cols.rearrange("(p j) m -> p j m", j=PACK))
 
+        load_weight("e", 0)
         for q in range(P // QUAD):
             nc.sync.dma_start(
                 out=x_plane[QUAD * q : QUAD * q + 4, :].bitcast(I32),
                 in_=x_scales[0, 4 * q : 4 * q + 4, :].bitcast(I32),
             )
-        load_weight("e", 0)
         nc.sync.dma_start(
             out=x_codes[:].bitcast(I32), in_=x_words[0].rearrange("p n t -> p (n t)").bitcast(I32)
         )
@@ -188,14 +188,14 @@ def tile_picked_wgatedg_none_lo_kernel(
             copy(out=tile[:], in_=sums[b, c])
             exact[b, c] = tile[:]
 
-        def store_rows(b, chunks):
+        def store_rows(b, chunks, copy):
             width = len(chunks) * P
             first = chunks[0] * P
             row_bank = psum.tile([P, width], F32, tag="bank", bufs=4)
             for i, c in enumerate(chunks):
                 nc.tensor.transpose(row_bank[:, i * P : (i + 1) * P], exact[b, c], ident[:])
             z_rows = work.tile([P, width], F32)
-            nc.scalar.copy(out=z_rows[:], in_=row_bank[:])
+            copy(out=z_rows[:], in_=row_bank[:])
             nc.sync.dma_start(out=out_0[b * P : (b + 1) * P, first : first + width], in_=z_rows[:])
 
         def requantize(c, word_copy):
@@ -253,7 +253,7 @@ def tile_picked_wgatedg_none_lo_kernel(
                 elif d >= 2 and b < last:
                     block_message(b, d - 2)
                 elif d >= 2:
-                    last_message(d - 2, every if d == 2 else every[:-1])
+                    last_message(d - 2, every[:-1])
                 if b < last:
                     if d == 0:
                         round_weights("ey", b + 1, nc.scalar.copy)
@@ -272,7 +272,7 @@ def tile_picked_wgatedg_none_lo_kernel(
                 if b > 0 and d == 2:
                     drain_block(b - 1)
                 if b > 0 and d == 3:
-                    store_rows(b - 1, every)
+                    store_rows(b - 1, every, nc.scalar.copy)
 
         last_message(2, [0, 1])
         last_message(3, [0, 1])
@@ -285,17 +285,16 @@ def tile_picked_wgatedg_none_lo_kernel(
         requantize(1, nc.scalar.copy)
         drain_pairs(last, 2)
         drain_exact(last, 2, nc.scalar.copy)
-        last_message(1, [3])
-        last_message(2, [3])
-        last_message(3, [3])
-        requantize(2, nc.vector.tensor_copy)
-        store_rows(last, [0, 1, 2])
+        for d in range(D):
+            last_message(d, [3])
+        requantize(2, nc.scalar.copy)
+        store_rows(last, [0, 1, 2], nc.vector.tensor_copy)
         store_words([0, 1, 2])
         drain_pairs(last, 3)
-        drain_exact(last, 3, nc.vector.tensor_copy)
+        drain_exact(last, 3, nc.scalar.copy)
         requantize(3, nc.scalar.copy)
         store_words([3])
-        store_rows(last, [3])
+        store_rows(last, [3], nc.scalar.copy)
         for q in range(P // QUAD):
             queue = nc.sync if q % 2 else nc.scalar
             queue.dma_start(

from contextlib import ExitStack

import concourse.mybir as mybir
from concourse.masks import make_identity

K, T, N, D = 512, 512, 512, 4
FLOPS = 3 * 2 * K * T * N

F32 = mybir.dt.float32
BF16 = mybir.dt.bfloat16
I32 = mybir.dt.int32
U32 = mybir.dt.uint32
U16 = mybir.dt.uint16
U8 = mybir.dt.uint8
FP8X4 = mybir.dt.float8_e4m3fn_x4
ADD = mybir.AluOpType.add
MULT = mybir.AluOpType.mult
SIGMOID = mybir.ActivationFunctionType.Sigmoid

P = 128
PACK = 4
BLOCKS = N // P
CHUNKS = T // P
SPARE = 8
QUAD = 32
HALF = T // 2
ROUND_SLOT = {("h", 0): "slot_a", ("ey", 1): "slot_b"}
CODES_SLOT = {("y", 0): "slot_a", ("h", 0): "slot_b"}


def tile_picked_wgatedg_none_lo_kernel(
    tc, x_words, x_scales, w1, w2, w3, pos1, pos2, pos3, pos4, out_0, out_1, out_2
):
    nc = tc.nc
    with ExitStack() as ctx:
        keep = ctx.enter_context(tc.tile_pool(name="keep", bufs=1))
        work = ctx.enter_context(tc.tile_pool(name="work", bufs=2))
        psum = ctx.enter_context(tc.psum_pool(name="psum", bufs=1))

        x_codes = keep.tile([P, T], U32, align_bytes=64)
        x_plane = keep.tile([P, T], U8, align_bytes=64)
        lists = [keep.tile([P, T // 16], U16, name="list%d" % d) for d in range(D)]
        weights = {"e": w2, "y": w1, "h": w3}
        raw = {}
        for b in range(BLOCKS):
            for part in weights:
                raw[part, b] = keep.tile([P, PACK, P], F32, name="raw_%s%d" % (part, b))

        def load_weight(part, b):
            cols = weights[part][:, b * P : (b + 1) * P]
            nc.sync.dma_start(out=raw[part, b][:], in_=cols.rearrange("(p j) m -> p j m", j=PACK))

        load_weight("e", 0)
        for q in range(P // QUAD):
            nc.sync.dma_start(
                out=x_plane[QUAD * q : QUAD * q + 4, :].bitcast(I32),
                in_=x_scales[0, 4 * q : 4 * q + 4, :].bitcast(I32),
            )
        nc.sync.dma_start(
            out=x_codes[:].bitcast(I32), in_=x_words[0].rearrange("p n t -> p (n t)").bitcast(I32)
        )
        load_weight("y", 0)
        nc.sync.dma_start(lists[0][:], pos1)
        load_weight("h", 0)
        nc.sync.dma_start(lists[1][:], pos2)
        nc.sync.dma_start(lists[2][:], pos3)
        nc.sync.dma_start(lists[3][:], pos4)
        for b in range(1, BLOCKS):
            for part in weights:
                load_weight(part, b)

        ident = keep.tile([P, P], F32)
        make_identity(nc, ident[:])

        proj = {}
        for b in range(BLOCKS):
            proj["y", b] = keep.tile([P, T], F32, name="y%d" % b)
            for part in ("e", "h"):
                proj[part, b] = keep.tile([P, T + SPARE], F32, name="%s%d" % (part, b))

        z_codes = keep.tile([P, T], U32, align_bytes=64)
        z_plane = keep.tile([P, T], U8, align_bytes=64)
        pairs = keep.tile([P, CHUNKS, 2, P, 2], BF16)


        rounded = {}
        quantized = {}
        products = {}

        def round_weights(parts, b, copy):
            grouped = keep.tile([P, len(parts), P, PACK], BF16, align_bytes=64, tag=ROUND_SLOT.get((parts, b), "rounded_%s%d" % (parts, b)))
            for i, part in enumerate(parts):
                copy(
                    out=grouped[:, i].rearrange("p (c i) j -> p c j i", i=4),
                    in_=raw[part, b][:].rearrange("p j (c i) -> p c j i", i=4),
                )
            rounded[parts, b] = grouped

        def quantize_weights(parts, b):
            w_codes = keep.tile([P, len(parts) * P], U32, align_bytes=64, tag=CODES_SLOT.get((parts, b), "codes_%s%d" % (parts, b)))
            w_plane = work.tile([P, len(parts) * P], U8, align_bytes=64, bufs=9)
            nc.vector.quantize_mx(
                out=w_codes[:].bitcast(FP8X4),
                scales=w_plane[:],
                in_=rounded[parts, b][:].rearrange("p i c j -> p (i c j)"),
            )
            for i, part in enumerate(parts):
                quantized[part, b] = (w_codes[:, i * P : (i + 1) * P], w_plane[:, i * P : (i + 1) * P])

        def multiply(part, b, cols):
            w_codes, w_plane = quantized[part, b]
            acc = psum.tile([P, cols.stop - cols.start], F32, tag="bank", bufs=4)
            nc.tensor.matmul_mx(
                out=acc[:],
                lhsT=w_codes.bitcast(FP8X4),
                lhsT_scale=w_plane,
                rhs=x_codes[:, cols].bitcast(FP8X4),
                rhs_scale=x_plane[:, cols],
                start=True,
                stop=True,
            )
            products[part, b, cols.start] = acc

        def unload(part, b, cols, copy):
            copy(out=proj[part, b][:, cols], in_=products[part, b, cols.start][:])

        def offsets(d, cols):
            return lists[d][:, cols.start // 16 : cols.stop // 16]

        gates = {}
        messages = {}
        sums = {}

        def gate(b, d, pieces):
            logit = work.tile([P, T], F32, bufs=3)
            for cols in pieces:
                nc.vector.tensor_tensor(
                    logit[:, cols], proj["e", b][:].indirect(offsets(d, cols)), proj["y", b][:, cols], ADD
                )
            gates[b, d] = work.tile([P, T], F32, bufs=4, name="gate")
            nc.scalar.activation(gates[b, d][:], logit[:], SIGMOID)

        def message(b, d, chunks):
            cols = slice(chunks[0] * P, (chunks[-1] + 1) * P)
            msg = work.tile([P, len(chunks) * P], F32, bufs=20)
            nc.vector.tensor_tensor(
                msg[:], proj["h", b][:].indirect(offsets(d, cols)), gates[b, d][:, cols], MULT
            )
            for i, c in enumerate(chunks):
                messages[b, d, c] = msg[:, i * P : (i + 1) * P]
            return msg

        def accumulate(b, d, c, start, stop):
            nc.tensor.matmul(sums[b, c], messages[b, d, c], ident[:], start=start, stop=stop, is_transpose=True)

        def block_message(b, d):
            message(b, d, every)
            if d == D - 2:
                sums[b] = psum.tile([P, CHUNKS, P], F32, name="sum%d" % (b + 1))
                for turn in (d, 0, 1):
                    for c in range(CHUNKS):
                        sums[b, c] = sums[b][:, c, :]
                        accumulate(b, turn, c, turn == d and c == 0, False)
            if d == D - 1:
                for c in range(CHUNKS):
                    accumulate(b, d, c, False, c == CHUNKS - 1)

        exact = {}

        def drain_block(b):
            tile = work.tile([P, CHUNKS, P], F32, name="exact_block")
            nc.scalar.copy(out=tile[:], in_=sums[b][:])
            for c in range(CHUNKS):
                exact[b, c] = tile[:, c, :]
            nc.scalar.copy(
                out=pairs[:, :, :, QUAD * b : QUAD * (b + 1), :],
                in_=sums[b][:].rearrange("v c (l u e) -> v c u l e", u=2, e=2),
            )

        def drain_pairs(b, c):
            nc.scalar.copy(
                out=pairs[:, c, :, QUAD * b : QUAD * (b + 1), :],
                in_=sums[b, c].rearrange("v (l u e) -> v u l e", u=2, e=2),
            )

        def drain_exact(b, c, copy):
            tile = work.tile([P, P], F32, name="exact_chunk", bufs=4)
            copy(out=tile[:], in_=sums[b, c])
            exact[b, c] = tile[:]

        def store_rows(b, chunks, copy):
            width = len(chunks) * P
            first = chunks[0] * P
            row_bank = psum.tile([P, width], F32, tag="bank", bufs=4)
            for i, c in enumerate(chunks):
                nc.tensor.transpose(row_bank[:, i * P : (i + 1) * P], exact[b, c], ident[:])
            z_rows = work.tile([P, width], F32)
            copy(out=z_rows[:], in_=row_bank[:])
            nc.sync.dma_start(out=out_0[b * P : (b + 1) * P, first : first + width], in_=z_rows[:])

        def requantize(c, word_copy):
            pair_words = pairs[:, c].rearrange("v u l e -> v u (l e)").bitcast(F32)
            word_bank = psum.tile([P, 2, P], F32, tag="bank", bufs=4)
            for u in range(2):
                nc.tensor.transpose(word_bank[:, u, :], pair_words[:, u, :], ident[:])
            z_grouped = work.tile([P, P * PACK], BF16, align_bytes=64, bufs=4)
            word_copy(
                out=z_grouped[:].bitcast(F32).rearrange("p (v u) -> p v u", u=2),
                in_=word_bank[:].rearrange("p u v -> p v u"),
            )
            cols = slice(c * P, (c + 1) * P)
            nc.vector.quantize_mx(out=z_codes[:, cols].bitcast(FP8X4), scales=z_plane[:, cols], in_=z_grouped[:])

        out_words = out_1[0].rearrange("l v t -> l (v t)").bitcast(I32)

        def store_words(chunks):
            cols = slice(chunks[0] * P, (chunks[-1] + 1) * P)
            nc.sync.dma_start(out=out_words[:, cols], in_=z_codes[:, cols].bitcast(I32))

        whole = slice(0, T)
        halves = [slice(0, HALF), slice(HALF, T)]
        every = list(range(CHUNKS))
        last = BLOCKS - 1

        round_weights("e", 0, nc.vector.tensor_copy)
        quantize_weights("e", 0)
        round_weights("y", 0, nc.vector.tensor_copy)
        quantize_weights("y", 0)
        multiply("e", 0, whole)
        unload("e", 0, whole, nc.scalar.copy)
        for cols in halves:
            multiply("y", 0, cols)
            unload("y", 0, cols, nc.scalar.copy)

        def last_message(d, chunks):
            msg = message(last, d, chunks)
            for c in chunks:
                if d == 0:
                    sums[last, c] = psum.tile([P, P], F32, name="sum%d" % c)[:]
                accumulate(last, d, c, d == 0, d == D - 1)
            return msg

        for b in range(BLOCKS):
            for d in range(D):
                gate(b, d, halves if b == 0 and d == 0 else [whole])
                if b == 0 and d == 0:
                    round_weights("h", 0, nc.scalar.copy)
                    quantize_weights("h", 0)
                    multiply("h", 0, whole)
                    unload("h", 0, whole, nc.scalar.copy)
                if d < 2 and b > 0:
                    block_message(b - 1, d + 2)
                elif d >= 2 and b < last:
                    block_message(b, d - 2)
                elif d >= 2:
                    last_message(d - 2, every[:-1])
                if b < last:
                    if d == 0:
                        round_weights("ey", b + 1, nc.scalar.copy)
                    if d == 1:
                        quantize_weights("ey", b + 1)
                        multiply("e", b + 1, whole)
                        multiply("y", b + 1, whole)
                        round_weights("h", b + 1, nc.scalar.copy)
                    if d == 2:
                        unload("e", b + 1, whole, nc.scalar.copy)
                        unload("y", b + 1, whole, nc.scalar.copy)
                        quantize_weights("h", b + 1)
                        multiply("h", b + 1, whole)
                    if d == 3:
                        unload("h", b + 1, whole, nc.scalar.copy)
                if b > 0 and d == 2:
                    drain_block(b - 1)
                if b > 0 and d == 3:
                    store_rows(b - 1, every, nc.scalar.copy)

        last_message(2, [0, 1])
        last_message(3, [0, 1])
        for c in (0, 1):
            drain_pairs(last, c)
            drain_exact(last, c, nc.scalar.copy)
        last_message(2, [2])
        last_message(3, [2])
        requantize(0, nc.scalar.copy)
        requantize(1, nc.scalar.copy)
        drain_pairs(last, 2)
        drain_exact(last, 2, nc.scalar.copy)
        for d in range(D):
            last_message(d, [3])
        requantize(2, nc.scalar.copy)
        store_rows(last, [0, 1, 2], nc.vector.tensor_copy)
        store_words([0, 1, 2])
        drain_pairs(last, 3)
        drain_exact(last, 3, nc.scalar.copy)
        requantize(3, nc.scalar.copy)
        store_words([3])
        store_rows(last, [3], nc.scalar.copy)
        for q in range(P // QUAD):
            queue = nc.sync if q % 2 else nc.scalar
            queue.dma_start(
                out=out_2[0, 4 * q : 4 * q + 4, :].bitcast(I32),
                in_=z_plane[QUAD * q : QUAD * q + 4, :].bitcast(I32),
            )
